import numpy as np
import ml_dtypes


def mxq(x, axis, fmt="e4m3"):
    dtype, down = {"e4m3": (ml_dtypes.float8_e4m3fn, 7), "e5m2": (ml_dtypes.float8_e5m2, 14)}[fmt]
    v = np.moveaxis(np.asarray(x, np.float32).astype(ml_dtypes.bfloat16).astype(np.float64), axis, -1)
    blocks = v.reshape(v.shape[:-1] + (-1, 32))
    amax = np.abs(blocks).max(-1, keepdims=True)
    byte = np.maximum(np.where(amax > 0, np.frexp(amax)[1] - 1 + 127, 0) - down, 1)
    scale = np.exp2(byte - 127.0)
    codes = (blocks / scale).astype(np.float32).astype(dtype).astype(np.float64)
    return np.moveaxis((codes * scale).reshape(v.shape), -1, axis)


WIDE = False


def mx_kscale(k):
    if not WIDE:
        return np.ones(k)
    levels = np.array([30, -30])
    if k % 512:
        return np.exp2(np.random.permutation(np.resize(levels, k // 32))).repeat(32)
    a = np.empty((k // 512, 16))
    for p in range(k // 512):
        a[p, :8] = np.random.permutation(np.resize(levels, 8))
        for g in range(8):
            far = levels[np.abs(levels - a[p, g]) >= 10]
            a[p, g + 8] = far[np.random.randint(len(far))]
    return np.exp2(a.ravel()).repeat(32)


def f64(x):
    return np.asarray(x).astype(np.float64)


def striped(idx):
    return np.tile(np.asarray(idx).reshape(-1, 16).T, (8, 1)).astype(np.uint16)


def unstriped(offs):
    return offs[:16].T.reshape(-1).astype(np.int64)


def striped8(idx):
    return np.asarray(idx).reshape(8, -1, 16).transpose(0, 2, 1).reshape(128, -1).astype(np.uint16)


def unstriped8(offs):
    return offs.reshape(8, 16, -1).transpose(0, 2, 1).reshape(8, -1).astype(np.int64)


def pick8(x, idx, run):
    r = np.arange(len(x))
    return x[r[:, None], idx[r % (8 * run) // run]]


E2M1 = np.array([0.0, 0.5, 1.0, 1.5, 2.0, 3.0, 4.0, 6.0, -0.0, -0.5, -1.0, -1.5, -2.0, -3.0, -4.0, -6.0])


def pack_weight(w, fmt):
    k, n = w.shape
    w = f64(np.asarray(w, np.float32).astype(ml_dtypes.bfloat16)).reshape(k // 32, 32, n)
    amax = np.abs(w).max(1)
    if fmt in ("e4m3", "e5m2"):
        byte = np.frexp(amax)[1] - 1 + 127 - (7 if fmt == "e4m3" else 14)
    else:
        mant, ex = np.frexp(amax / 6.0)
        byte = np.where(mant > 0.5, ex, ex - 1) + 127
    byte = np.clip(np.where(amax > 0, byte, 1), 1, 254)
    scaled = (w * np.exp2(127.0 - byte)[:, None, :]).reshape(k, n).astype(np.float32)
    by_word = np.ascontiguousarray(scaled.reshape(k // 512, 128, 4, n).transpose(0, 1, 3, 2))
    if fmt in ("e4m3", "e5m2"):
        words = by_word.astype(ml_dtypes.float8_e4m3fn if fmt == "e4m3" else ml_dtypes.float8_e5m2).view(np.uint8)
    else:
        c = by_word.astype(ml_dtypes.float4_e2m1fn).view(np.uint8) & 0xF
        words = (c[..., 0::2] | (c[..., 1::2] << 4)).reshape(k // 512, 128, 2 * n)
    return np.ascontiguousarray(words), np.ascontiguousarray(byte.astype(np.uint8).reshape(k // 512, 16, n))


def unpack_weight(words, scales, fmt):
    g, _, n = scales.shape
    words = np.ascontiguousarray(words).reshape(g, 128, n, -1)
    if fmt in ("e4m3", "e5m2"):
        vals = words.view(ml_dtypes.float8_e4m3fn if fmt == "e4m3" else ml_dtypes.float8_e5m2).astype(np.float64)
    else:
        nib = np.empty((g, 128, n, 4), np.uint8)
        nib[..., 0::2] = words & 0xF
        nib[..., 1::2] = words >> 4
        vals = E2M1[nib]
    vals = vals * np.repeat(np.exp2(scales.astype(np.float64) - 127.0), 8, axis=1)[..., None]
    return vals.transpose(0, 1, 3, 2).reshape(g * 512, n)


K, T, J, R, V, C, N = 512, 1024, 256, 512, 1024, 512, 256


def setup_inputs():
    n = np.random.standard_normal
    idx = np.random.permutation(V)[:R]
    idx2 = np.random.permutation(T)[:J]
    idx3 = np.stack([np.random.permutation(C)[:J] for _ in range(8)])
    idx4 = np.random.permutation(C)[:J]
    idx5 = np.random.permutation(C)[:J]
    fk = mx_kscale(K)
    fr = mx_kscale(R)
    tr = np.ones(V)
    tr[idx] = fr
    xtp = pack_weight(n((K, T)) / fk[:, None], "e4m3")
    wtp = pack_weight(n((K, V)) * 1 / np.sqrt(K) * fk[:, None] * tr, "e2m1")
    wbp = pack_weight(n((R, N)) * 1 / np.sqrt(R) / fr[:, None], "e5m2")
    return {
        "xt_words": xtp[0],
        "xt_scales": xtp[1],
        "wt_words": wtp[0],
        "wt_scales": wtp[1],
        "wb_words": wbp[0],
        "wb_scales": wbp[1],
        "offs": striped(idx),
        "offs2": striped(idx2),
        "offs3": striped8(idx3),
        "offs4": striped(idx4),
        "offs5": striped(idx5),
    }


def reference(xt_words, xt_scales, wt_words, wt_scales, wb_words, wb_scales, offs, offs2, offs3, offs4, offs5):
    idx = unstriped(offs)
    idx2 = unstriped(offs2)
    idx3 = unstriped8(offs3)
    idx4 = unstriped(offs4)
    idx5 = unstriped(offs5)
    xtu = unpack_weight(xt_words, xt_scales, "e4m3")
    wtu = unpack_weight(wt_words, wt_scales, "e2m1")
    wbu = unpack_weight(wb_words, wb_scales, "e5m2")
    wtidxg = wtu[:, idx]
    xtidx2g = xtu[:, idx2]
    a = wtidxg.T @ xtidx2g
    pa = np.zeros((R, C))
    pa[np.arange(R)[:, None], idx3[np.arange(R) % 512 // 64]] = a
    hid = np.minimum(np.abs(pa[:, idx4] - a), np.abs(pa[:, idx5] - a))
    hidq = mxq(hid, 0, "e4m3")
    p = wbu.T @ hidq
    return p

@@ -1,0 +1,170 @@
+from contextlib import ExitStack
+
+import concourse.mybir as mybir
+
+K, T, J, R, V, C, N = 512, 1024, 256, 512, 1024, 512, 256
+FLOPS = 2 * K * R * J + 2 * R * N * J
+
+F32 = mybir.dt.float32
+BF16 = mybir.dt.bfloat16
+I32 = mybir.dt.int32
+U32 = mybir.dt.uint32
+U16 = mybir.dt.uint16
+U8 = mybir.dt.uint8
+E4M3 = mybir.dt.float8_e4m3fn_x4
+E5M2 = mybir.dt.float8_e5m2_x4
+E2M1 = mybir.dt.float4_e2m1fn_x4
+ALU = mybir.AluOpType
+ACT = mybir.ActivationFunctionType
+
+P = 128
+PACK = 4
+HALF = J // 2
+
+
+def load_scale_rows(queue, plane, scales):
+    for q in range(4):
+        queue.dma_start(out=plane[32 * q : 32 * q + 4, :].bitcast(I32), in_=scales[0, 4 * q : 4 * q + 4, :].bitcast(I32))
+
+
+def tile_list_nearerpost_kernel(
+    tc, xt_words, xt_scales, wt_words, wt_scales, wb_words, wb_scales, offs, offs2, offs3, offs4, offs5, out
+):
+    nc = tc.nc
+    with ExitStack() as ctx:
+        sb = ctx.enter_context(tc.tile_pool(name="sb", bufs=1))
+        ring = ctx.enter_context(tc.tile_pool(name="ring", bufs=2))
+        ps = ctx.enter_context(tc.psum_pool(name="ps", bufs=1))
+
+        def tile(name, shape, dtype):
+            return sb.tile(shape, dtype, name=name, align_bytes=64)
+
+        l1 = tile("l1", [P, R // 16], U16)
+        l2 = tile("l2", [P, J // 16], U16)
+        l3 = tile("l3", [P, J // 16], U16)
+        l4 = tile("l4", [P, J // 16], U16)
+        l5 = tile("l5", [P, J // 16], U16)
+        wt_w = tile("wt_w", [P, V], U16)
+        wt_s = tile("wt_s", [P, V], U8)
+        xt_w = tile("xt_w", [P, T], U32)
+        xt_s = tile("xt_s", [P, T], U8)
+        wb_w = tile("wb_w", [P, N], U32)
+        wb_s = tile("wb_s", [P, N], U8)
+        board = [tile("board%d" % t, [P, C], F32) for t in range(PACK)]
+
+        nc.gpsimd.memset(wt_s[:].bitcast(I32), 0)
+        nc.vector.memset(xt_s[:].bitcast(I32), 0)
+        nc.vector.memset(wb_s[:].bitcast(I32), 0)
+        for t in range(PACK):
+            nc.vector.memset(board[t][:], 0.0)
+
+        nc.sync.dma_start(out=l1[:], in_=offs)
+        nc.scalar.dma_start(out=wt_w[:].bitcast(I32), in_=wt_words[0].bitcast(I32))
+        load_scale_rows(nc.sync, wt_s, wt_scales)
+        nc.scalar.dma_start(out=xt_w[:].bitcast(I32), in_=xt_words[0].rearrange("p n t -> p (n t)").bitcast(I32))
+        nc.sync.dma_start(out=l2[:], in_=offs2)
+        load_scale_rows(nc.sync, xt_s, xt_scales)
+        nc.sync.dma_start(out=l3[:], in_=offs3)
+        nc.sync.dma_start(out=l4[:], in_=offs4)
+        nc.sync.dma_start(out=l5[:], in_=offs5)
+        nc.sync.dma_start(out=wb_w[:].bitcast(I32), in_=wb_words[0].rearrange("p n t -> p (n t)").bitcast(I32))
+        load_scale_rows(nc.sync, wb_s, wb_scales)
+
+        wg_s = tile("wg_s", [P, R], U8)
+        wg_w = tile("wg_w", [P, R], U16)
+        wd_s = tile("wd_s", [P, R], U8)
+        wd_w = tile("wd_w", [P, R], U16)
+        xg_w = tile("xg_w", [P, J], U32)
+        xg_s = tile("xg_s", [P, J], U8)
+
+        nc.vector.tensor_copy(out=wg_s[:], in_=wt_s[:].indirect(l1[:]))
+        nc.vector.tensor_copy(out=wg_w[:], in_=wt_w[:].indirect(l1[:]))
+        hc = HALF // 16
+
+        def deal(ts):
+            nc.vector.tensor_copy(
+                out=wd_s[:].rearrange("p (t b i) -> p b t i", t=PACK, i=16)[:, :, ts, :],
+                in_=wg_s[:].rearrange("p (b i t) -> p b t i", t=PACK, i=16)[:, :, ts, :],
+            )
+            nc.vector.tensor_copy(
+                out=wd_w[:].rearrange("p (t b i) -> p b t i", t=PACK, i=8)[:, :, ts, :],
+                in_=wg_w[:].rearrange("p (b i t) -> p b t i", t=PACK, i=8)[:, :, ts, :],
+            )
+
+        deal(slice(0, 1))
+        nc.vector.tensor_copy(out=xg_w[:], in_=xt_w[:].indirect(l2[:]))
+        nc.vector.tensor_copy(out=xg_s[:], in_=xt_s[:].indirect(l2[:]))
+        deal(slice(1, PACK))
+
+        def first_product(bank, t, cols):
+            nc.tensor.matmul_mx(
+                out=bank,
+                lhsT=wd_w[:, t * P : (t + 1) * P].bitcast(E2M1),
+                lhsT_scale=wd_s[:, t * P : (t + 1) * P],
+                rhs=xg_w[:, cols].bitcast(E4M3),
+                rhs_scale=xg_s[:, cols],
+                start=True,
+                stop=True,
+            )
+
+        a = [tile("a%d" % t, [P, J], F32) for t in range(PACK)]
+        for t in range(PACK):
+            bank = ps.tile([P, J], F32, name="a%d" % t)
+            first_product(bank[:], t, slice(0, J))
+            nc.vector.tensor_copy(out=a[t][:], in_=bank[:])
+            nc.scalar.activation(out=board[t][:].indirect(l3[:]), in_=a[t][:], func=ACT.Copy)
+
+        mag = tile("mag", [P, PACK, 2 * J], F32)
+        last = PACK - 1
+        for t in range(last):
+            diff = ring.tile([P, 2, J], F32, name="diff")
+            for s, lst in enumerate((l4, l5)):
+                nc.vector.tensor_tensor(out=diff[:, s, :], in0=board[t][:].indirect(lst[:]), in1=a[t][:], op=ALU.subtract)
+            flat = diff[:].rearrange("p s j -> p (s j)")
+            if t < 2:
+                nc.vector.scalar_tensor_tensor(out=mag[:, t, :], in0=flat, scalar=-1.0, in1=flat, op0=ALU.mult, op1=ALU.max)
+            else:
+                nc.scalar.activation(out=mag[:, t, :], in_=flat, func=ACT.Abs)
+        diff = ring.tile([P, 2, J], F32, name="diff")
+        for h in range(2):
+            cols = slice(h * HALF, (h + 1) * HALF)
+            for s, lst in enumerate((l4, l5)):
+                nc.vector.tensor_tensor(
+                    out=diff[:, s, cols],
+                    in0=board[last][:].indirect(lst[:, h * hc : (h + 1) * hc]),
+                    in1=a[last][:, cols],
+                    op=ALU.subtract,
+                )
+            nc.scalar.activation(
+                out=mag[:, last, :].rearrange("p (s j) -> p s j", s=2)[:, :, cols], in_=diff[:, :, cols], func=ACT.Abs
+            )
+
+        out_v = out.rearrange("(g p) j -> p g j", p=P)
+        for h in range(2):
+            hid = tile("hid%d" % h, [P, HALF * PACK], BF16)
+            near = [
+                mag[:, :, s * J + h * HALF : s * J + (h + 1) * HALF].rearrange("p t (b i) -> p b t i", i=4) for s in range(2)
+            ]
+            nc.vector.tensor_tensor(
+                out=hid[:].rearrange("p (b i t) -> p b t i", t=PACK, i=4), in0=near[0], in1=near[1], op=ALU.min
+            )
+            hq_w = tile("hq_w%d" % h, [P, HALF], U32)
+            hq_s = tile("hq_s%d" % h, [P, HALF], U8)
+            nc.vector.quantize_mx(out=hq_w[:].bitcast(E4M3), scales=hq_s[:], in_=hid[:])
+            for g in range(2):
+                res = tile("res%d%d" % (h, g), [P, HALF], F32)
+                bank = ps.tile([P, HALF], F32, name="o%d%d" % (h, g))
+                nc.tensor.matmul_mx(
+                    out=bank[:],
+                    lhsT=wb_w[:, g * P : (g + 1) * P].bitcast(E5M2),
+                    lhsT_scale=wb_s[:, g * P : (g + 1) * P],
+                    rhs=hq_w[:].bitcast(E4M3),
+                    rhs_scale=hq_s[:],
+                    start=True,
+                    stop=True,
+                )
+                if h == 1 and g == 0:
+                    nc.vector.tensor_copy(out=res[:], in_=bank[:])
+                else:
+                    nc.scalar.copy(out=res[:], in_=bank[:])
+                (nc.sync if g == 0 else nc.scalar).dma_start(out=out_v[:, g, h * HALF : (h + 1) * HALF], in_=res[:])

@@ -27,17 +27,23 @@ def load_scale_rows(queue, plane, scales):
         queue.dma_start(out=plane[32 * q : 32 * q + 4, :].bitcast(I32), in_=scales[0, 4 * q : 4 * q + 4, :].bitcast(I32))
 
 
+def load_scale_window(queues, plane, scales):
+    for q in range(4):
+        queue = queues[q % len(queues)]
+        rows = scales[:, 4 * q : 4 * q + 4, :].bitcast(I32)
+        queue.dma_start(out=plane[32 * q : 32 * q + 32, :].bitcast(I32), in_=rows.to_broadcast([8, 4, rows.shape[2]]))
+
+
 def tile_list_nearerpost_kernel(
     tc, xt_words, xt_scales, wt_words, wt_scales, wb_words, wb_scales, offs, offs2, offs3, offs4, offs5, out
 ):
     nc = tc.nc
     with ExitStack() as ctx:
         sb = ctx.enter_context(tc.tile_pool(name="sb", bufs=1))
-        ring = ctx.enter_context(tc.tile_pool(name="ring", bufs=2))
         ps = ctx.enter_context(tc.psum_pool(name="ps", bufs=1))
 
-        def tile(name, shape, dtype):
-            return sb.tile(shape, dtype, name=name, align_bytes=64)
+        def tile(name, shape, dtype, tag=None):
+            return sb.tile(shape, dtype, name=name, tag=tag or name, align_bytes=64)
 
         l1 = tile("l1", [P, R // 16], U16)
         l2 = tile("l2", [P, J // 16], U16)
@@ -52,18 +58,16 @@ def tile_list_nearerpost_kernel(
         wb_s = tile("wb_s", [P, N], U8)
         board = [tile("board%d" % t, [P, C], F32) for t in range(PACK)]
 
-        nc.gpsimd.memset(wt_s[:].bitcast(I32), 0)
-        nc.vector.memset(xt_s[:].bitcast(I32), 0)
         nc.vector.memset(wb_s[:].bitcast(I32), 0)
         for t in range(PACK):
-            nc.vector.memset(board[t][:], 0.0)
+            (nc.vector if t < 2 else nc.gpsimd).memset(board[t][:], 0.0)
 
         nc.sync.dma_start(out=l1[:], in_=offs)
+        load_scale_window((nc.scalar, nc.sync), wt_s, wt_scales)
         nc.scalar.dma_start(out=wt_w[:].bitcast(I32), in_=wt_words[0].bitcast(I32))
-        load_scale_rows(nc.sync, wt_s, wt_scales)
-        nc.scalar.dma_start(out=xt_w[:].bitcast(I32), in_=xt_words[0].rearrange("p n t -> p (n t)").bitcast(I32))
         nc.sync.dma_start(out=l2[:], in_=offs2)
-        load_scale_rows(nc.sync, xt_s, xt_scales)
+        nc.sync.dma_start(out=xt_w[:].bitcast(I32), in_=xt_words[0].rearrange("p n t -> p (n t)").bitcast(I32))
+        load_scale_window((nc.sync,), xt_s, xt_scales)
         nc.sync.dma_start(out=l3[:], in_=offs3)
         nc.sync.dma_start(out=l4[:], in_=offs4)
         nc.sync.dma_start(out=l5[:], in_=offs5)
@@ -77,24 +81,23 @@ def tile_list_nearerpost_kernel(
         xg_w = tile("xg_w", [P, J], U32)
         xg_s = tile("xg_s", [P, J], U8)
 
-        nc.vector.tensor_copy(out=wg_s[:], in_=wt_s[:].indirect(l1[:]))
-        nc.vector.tensor_copy(out=wg_w[:], in_=wt_w[:].indirect(l1[:]))
         hc = HALF // 16
 
-        def deal(ts):
+        def deal(dst, src, run, ts):
             nc.vector.tensor_copy(
-                out=wd_s[:].rearrange("p (t b i) -> p b t i", t=PACK, i=16)[:, :, ts, :],
-                in_=wg_s[:].rearrange("p (b i t) -> p b t i", t=PACK, i=16)[:, :, ts, :],
-            )
-            nc.vector.tensor_copy(
-                out=wd_w[:].rearrange("p (t b i) -> p b t i", t=PACK, i=8)[:, :, ts, :],
-                in_=wg_w[:].rearrange("p (b i t) -> p b t i", t=PACK, i=8)[:, :, ts, :],
+                out=dst[:].rearrange("p (t b i) -> p b t i", t=PACK, i=run)[:, :, ts, :],
+                in_=src[:].rearrange("p (b i t) -> p b t i", t=PACK, i=run)[:, :, ts, :],
             )
 
-        deal(slice(0, 1))
-        nc.vector.tensor_copy(out=xg_w[:], in_=xt_w[:].indirect(l2[:]))
-        nc.vector.tensor_copy(out=xg_s[:], in_=xt_s[:].indirect(l2[:]))
-        deal(slice(1, PACK))
+        nc.vector.tensor_copy(out=wg_s[:], in_=wt_s[:].indirect(l1[:]))
+        nc.vector.tensor_copy(out=wg_w[:], in_=wt_w[:].indirect(l1[:]))
+        deal(wd_s, wg_s, 16, slice(0, 1))
+        deal(wd_w, wg_w, 8, slice(0, 1))
+        for h in range(2):
+            nc.vector.tensor_copy(out=xg_w[:, h * HALF : (h + 1) * HALF], in_=xt_w[:].indirect(l2[:, h * hc : (h + 1) * hc]))
+            nc.vector.tensor_copy(out=xg_s[:, h * HALF : (h + 1) * HALF], in_=xt_s[:].indirect(l2[:, h * hc : (h + 1) * hc]))
+        deal(wd_s, wg_s, 16, slice(1, PACK))
+        deal(wd_w, wg_w, 8, slice(1, PACK))
 
         def first_product(bank, t, cols):
             nc.tensor.matmul_mx(
@@ -107,43 +110,56 @@ def tile_list_nearerpost_kernel(
                 stop=True,
             )
 
-        a = [tile("a%d" % t, [P, J], F32) for t in range(PACK)]
-        for t in range(PACK):
+        a0 = tile("a0", [P, J], F32)
+        head = tile("head", [P, HALF], F32, tag="later")
+        banks = [ps.tile([P, HALF], F32, name="a0h%d" % h) for h in range(2)]
+        for h in range(2):
+            first_product(banks[h][:], 0, slice(h * HALF, (h + 1) * HALF))
+        nc.scalar.copy(out=head[:], in_=banks[0][:])
+        nc.scalar.activation(out=board[0][:].indirect(l3[:, :hc]), in_=head[:], func=ACT.Copy)
+        nc.vector.tensor_copy(out=a0[:, HALF:], in_=banks[1][:])
+        nc.scalar.activation(out=board[0][:].indirect(l3[:, hc:]), in_=a0[:, HALF:], func=ACT.Copy)
+        nc.vector.tensor_copy(out=a0[:, :HALF], in_=banks[0][:])
+        rest = tile("rest", [P, PACK - 1, J], F32, tag="later")
+        a = [a0[:]] + [rest[:, t, :] for t in range(PACK - 1)]
+        for t in range(1, PACK):
             bank = ps.tile([P, J], F32, name="a%d" % t)
             first_product(bank[:], t, slice(0, J))
-            nc.vector.tensor_copy(out=a[t][:], in_=bank[:])
-            nc.scalar.activation(out=board[t][:].indirect(l3[:]), in_=a[t][:], func=ACT.Copy)
+            nc.vector.tensor_copy(out=a[t], in_=bank[:])
+            nc.scalar.activation(out=board[t][:].indirect(l3[:]), in_=a[t], func=ACT.Copy)
 
-        mag = tile("mag", [P, PACK, 2 * J], F32)
+        mag = tile("mag", [P, PACK, 2, J], F32)
         last = PACK - 1
-        for t in range(last):
-            diff = ring.tile([P, 2, J], F32, name="diff")
-            for s, lst in enumerate((l4, l5)):
-                nc.vector.tensor_tensor(out=diff[:, s, :], in0=board[t][:].indirect(lst[:]), in1=a[t][:], op=ALU.subtract)
-            flat = diff[:].rearrange("p s j -> p (s j)")
-            if t < 2:
-                nc.vector.scalar_tensor_tensor(out=mag[:, t, :], in0=flat, scalar=-1.0, in1=flat, op0=ALU.mult, op1=ALU.max)
-            else:
-                nc.scalar.activation(out=mag[:, t, :], in_=flat, func=ACT.Abs)
-        diff = ring.tile([P, 2, J], F32, name="diff")
-        for h in range(2):
-            cols = slice(h * HALF, (h + 1) * HALF)
+
+        def differences(dst, t, h0, h1):
             for s, lst in enumerate((l4, l5)):
                 nc.vector.tensor_tensor(
-                    out=diff[:, s, cols],
-                    in0=board[last][:].indirect(lst[:, h * hc : (h + 1) * hc]),
-                    in1=a[last][:, cols],
+                    out=dst[:, s, h0 * HALF : h1 * HALF],
+                    in0=board[t][:].indirect(lst[:, h0 * hc : h1 * hc]),
+                    in1=a[t][:, h0 * HALF : h1 * HALF],
                     op=ALU.subtract,
                 )
-            nc.scalar.activation(
-                out=mag[:, last, :].rearrange("p (s j) -> p s j", s=2)[:, :, cols], in_=diff[:, :, cols], func=ACT.Abs
-            )
+
+        diff0 = tile("diff0", [P, 2, J], F32, tag="diff")
+        differences(diff0, 0, 0, 2)
+        flat = diff0[:].rearrange("p s j -> p (s j)")
+        nc.vector.scalar_tensor_tensor(
+            out=mag[:, 0].rearrange("p s j -> p (s j)"), in0=flat, scalar=-1.0, in1=flat, op0=ALU.mult, op1=ALU.max
+        )
+        diffs = tile("diffs", [P, PACK - 1, 2, J], F32, tag="diff")
+        for t in (1, 2):
+            differences(diffs[:, t - 1], t, 0, 2)
+        for h in range(2):
+            cols = slice(h * HALF, (h + 1) * HALF)
+            differences(diffs[:, last - 1], last, h, h + 1)
+            nc.scalar.activation(out=mag[:, 1:last, :, cols], in_=diffs[:, : last - 1, :, cols], func=ACT.Abs)
+            nc.scalar.activation(out=mag[:, last, :, cols], in_=diffs[:, last - 1, :, cols], func=ACT.Abs)
 
         out_v = out.rearrange("(g p) j -> p g j", p=P)
         for h in range(2):
             hid = tile("hid%d" % h, [P, HALF * PACK], BF16)
             near = [
-                mag[:, :, s * J + h * HALF : s * J + (h + 1) * HALF].rearrange("p t (b i) -> p b t i", i=4) for s in range(2)
+                mag[:, :, s, h * HALF : (h + 1) * HALF].rearrange("p t (b i) -> p b t i", i=4) for s in range(2)
             ]
             nc.vector.tensor_tensor(
                 out=hid[:].rearrange("p (b i t) -> p b t i", t=PACK, i=4), in0=near[0], in1=near[1], op=ALU.min
@@ -153,7 +169,7 @@ def tile_list_nearerpost_kernel(
             nc.vector.quantize_mx(out=hq_w[:].bitcast(E4M3), scales=hq_s[:], in_=hid[:])
             for g in range(2):
                 res = tile("res%d%d" % (h, g), [P, HALF], F32)
-                bank = ps.tile([P, HALF], F32, name="o%d%d" % (h, g))
+                bank = ps.tile([P, HALF], F32, name=("a0h0", "a0h1", "o0", "o1")[2 * h + g])
                 nc.tensor.matmul_mx(
                     out=bank[:],
                     lhsT=wb_w[:, g * P : (g + 1) * P].bitcast(E5M2),

@@ -40,6 +40,7 @@ def tile_list_nearerpost_kernel(
     nc = tc.nc
     with ExitStack() as ctx:
         sb = ctx.enter_context(tc.tile_pool(name="sb", bufs=1))
+        reuse = ctx.enter_context(tc.tile_pool(name="reuse", bufs=1))
         ps = ctx.enter_context(tc.psum_pool(name="ps", bufs=1))
 
         def tile(name, shape, dtype, tag=None):
@@ -53,11 +54,12 @@ def tile_list_nearerpost_kernel(
         wt_w = tile("wt_w", [P, V], U16)
         wt_s = tile("wt_s", [P, V], U8)
         xt_w = tile("xt_w", [P, T], U32)
-        xt_s = tile("xt_s", [P, T], U8)
+        xt_s = reuse.tile([P, T], U8, name="xt_s", align_bytes=64, offset=0)
         wb_w = tile("wb_w", [P, N], U32)
         wb_s = tile("wb_s", [P, N], U8)
         board = [tile("board%d" % t, [P, C], F32) for t in range(PACK)]
 
+        nc.vector.memset(xt_s[:].bitcast(I32), 0)
         nc.vector.memset(wb_s[:].bitcast(I32), 0)
         for t in range(PACK):
             (nc.vector if t < 2 else nc.gpsimd).memset(board[t][:], 0.0)
@@ -67,7 +69,7 @@ def tile_list_nearerpost_kernel(
         nc.scalar.dma_start(out=wt_w[:].bitcast(I32), in_=wt_words[0].bitcast(I32))
         nc.sync.dma_start(out=l2[:], in_=offs2)
         nc.sync.dma_start(out=xt_w[:].bitcast(I32), in_=xt_words[0].rearrange("p n t -> p (n t)").bitcast(I32))
-        load_scale_window((nc.sync,), xt_s, xt_scales)
+        load_scale_rows(nc.sync, xt_s, xt_scales)
         nc.sync.dma_start(out=l3[:], in_=offs3)
         nc.sync.dma_start(out=l4[:], in_=offs4)
         nc.sync.dma_start(out=l5[:], in_=offs5)
@@ -76,8 +78,6 @@ def tile_list_nearerpost_kernel(
 
         wg_s = tile("wg_s", [P, R], U8)
         wg_w = tile("wg_w", [P, R], U16)
-        wd_s = tile("wd_s", [P, R], U8)
-        wd_w = tile("wd_w", [P, R], U16)
         xg_w = tile("xg_w", [P, J], U32)
         xg_s = tile("xg_s", [P, J], U8)
 
@@ -85,25 +85,32 @@ def tile_list_nearerpost_kernel(
 
         def deal(dst, src, run, ts):
             nc.vector.tensor_copy(
-                out=dst[:].rearrange("p (t b i) -> p b t i", t=PACK, i=run)[:, :, ts, :],
+                out=dst[:].rearrange("p (t b i) -> p b t i", b=P // run, i=run),
                 in_=src[:].rearrange("p (b i t) -> p b t i", t=PACK, i=run)[:, :, ts, :],
             )
 
         nc.vector.tensor_copy(out=wg_s[:], in_=wt_s[:].indirect(l1[:]))
         nc.vector.tensor_copy(out=wg_w[:], in_=wt_w[:].indirect(l1[:]))
-        deal(wd_s, wg_s, 16, slice(0, 1))
-        deal(wd_w, wg_w, 8, slice(0, 1))
+        wd0_s = tile("wd0_s", [P, P], U8)
+        wd0_w = tile("wd0_w", [P, P], U16)
+        deal(wd0_s, wg_s, 16, slice(0, 1))
+        deal(wd0_w, wg_w, 8, slice(0, 1))
+        nc.vector.tensor_copy(out=xg_w[:], in_=xt_w[:].indirect(l2[:]))
         for h in range(2):
-            nc.vector.tensor_copy(out=xg_w[:, h * HALF : (h + 1) * HALF], in_=xt_w[:].indirect(l2[:, h * hc : (h + 1) * hc]))
             nc.vector.tensor_copy(out=xg_s[:, h * HALF : (h + 1) * HALF], in_=xt_s[:].indirect(l2[:, h * hc : (h + 1) * hc]))
-        deal(wd_s, wg_s, 16, slice(1, PACK))
-        deal(wd_w, wg_w, 8, slice(1, PACK))
+        others = (PACK - 1) * P
+        wdr_s = reuse.tile([P, others], U8, name="wdr_s", align_bytes=64, offset=0)
+        wdr_w = reuse.tile([P, others], U16, name="wdr_w", align_bytes=64, offset=others)
+        deal(wdr_s, wg_s, 16, slice(1, PACK))
+        deal(wdr_w, wg_w, 8, slice(1, PACK))
+        wd_s = [wd0_s[:]] + [wdr_s[:, t * P : (t + 1) * P] for t in range(PACK - 1)]
+        wd_w = [wd0_w[:]] + [wdr_w[:, t * P : (t + 1) * P] for t in range(PACK - 1)]
 
         def first_product(bank, t, cols):
             nc.tensor.matmul_mx(
                 out=bank,
-                lhsT=wd_w[:, t * P : (t + 1) * P].bitcast(E2M1),
-                lhsT_scale=wd_s[:, t * P : (t + 1) * P],
+                lhsT=wd_w[t].bitcast(E2M1),
+                lhsT_scale=wd_s[t],
                 rhs=xg_w[:, cols].bitcast(E4M3),
                 rhs_scale=xg_s[:, cols],
                 start=True,

@@ -65,8 +65,8 @@ def tile_list_nearerpost_kernel(
             (nc.vector if t < 2 else nc.gpsimd).memset(board[t][:], 0.0)
 
         nc.sync.dma_start(out=l1[:], in_=offs)
-        load_scale_window((nc.scalar, nc.sync), wt_s, wt_scales)
-        nc.scalar.dma_start(out=wt_w[:].bitcast(I32), in_=wt_words[0].bitcast(I32))
+        nc.sync.dma_start(out=wt_w[:].bitcast(I32), in_=wt_words[0].bitcast(I32))
+        load_scale_window((nc.sync,), wt_s, wt_scales)
         nc.sync.dma_start(out=l2[:], in_=offs2)
         nc.sync.dma_start(out=xt_w[:].bitcast(I32), in_=xt_words[0].rearrange("p n t -> p (n t)").bitcast(I32))
         load_scale_rows(nc.sync, xt_s, xt_scales)
@@ -89,12 +89,12 @@ def tile_list_nearerpost_kernel(
                 in_=src[:].rearrange("p (b i t) -> p b t i", t=PACK, i=run)[:, :, ts, :],
             )
 
-        nc.vector.tensor_copy(out=wg_s[:], in_=wt_s[:].indirect(l1[:]))
         nc.vector.tensor_copy(out=wg_w[:], in_=wt_w[:].indirect(l1[:]))
+        nc.vector.tensor_copy(out=wg_s[:], in_=wt_s[:].indirect(l1[:]))
         wd0_s = tile("wd0_s", [P, P], U8)
         wd0_w = tile("wd0_w", [P, P], U16)
-        deal(wd0_s, wg_s, 16, slice(0, 1))
         deal(wd0_w, wg_w, 8, slice(0, 1))
+        deal(wd0_s, wg_s, 16, slice(0, 1))
         nc.vector.tensor_copy(out=xg_w[:], in_=xt_w[:].indirect(l2[:]))
         for h in range(2):
             nc.vector.tensor_copy(out=xg_s[:, h * HALF : (h + 1) * HALF], in_=xt_s[:].indirect(l2[:, h * hc : (h + 1) * hc]))

from contextlib import ExitStack

import concourse.mybir as mybir

K, T, J, R, V, C, N = 512, 1024, 256, 512, 1024, 512, 256
FLOPS = 2 * K * R * J + 2 * R * N * J

F32 = mybir.dt.float32
BF16 = mybir.dt.bfloat16
I32 = mybir.dt.int32
U32 = mybir.dt.uint32
U16 = mybir.dt.uint16
U8 = mybir.dt.uint8
E4M3 = mybir.dt.float8_e4m3fn_x4
E5M2 = mybir.dt.float8_e5m2_x4
E2M1 = mybir.dt.float4_e2m1fn_x4
ALU = mybir.AluOpType
ACT = mybir.ActivationFunctionType

P = 128
PACK = 4
HALF = J // 2


def load_scale_rows(queue, plane, scales):
    for q in range(4):
        queue.dma_start(out=plane[32 * q : 32 * q + 4, :].bitcast(I32), in_=scales[0, 4 * q : 4 * q + 4, :].bitcast(I32))


def load_scale_window(queues, plane, scales):
    for q in range(4):
        queue = queues[q % len(queues)]
        rows = scales[:, 4 * q : 4 * q + 4, :].bitcast(I32)
        queue.dma_start(out=plane[32 * q : 32 * q + 32, :].bitcast(I32), in_=rows.to_broadcast([8, 4, rows.shape[2]]))


def tile_list_nearerpost_kernel(
    tc, xt_words, xt_scales, wt_words, wt_scales, wb_words, wb_scales, offs, offs2, offs3, offs4, offs5, out
):
    nc = tc.nc
    with ExitStack() as ctx:
        sb = ctx.enter_context(tc.tile_pool(name="sb", bufs=1))
        reuse = ctx.enter_context(tc.tile_pool(name="reuse", bufs=1))
        ps = ctx.enter_context(tc.psum_pool(name="ps", bufs=1))

        def tile(name, shape, dtype, tag=None):
            return sb.tile(shape, dtype, name=name, tag=tag or name, align_bytes=64)

        l1 = tile("l1", [P, R // 16], U16)
        l2 = tile("l2", [P, J // 16], U16)
        l3 = tile("l3", [P, J // 16], U16)
        l4 = tile("l4", [P, J // 16], U16)
        l5 = tile("l5", [P, J // 16], U16)
        wt_w = tile("wt_w", [P, V], U16)
        wt_s = tile("wt_s", [P, V], U8)
        xt_w = tile("xt_w", [P, T], U32)
        xt_s = reuse.tile([P, T], U8, name="xt_s", align_bytes=64, offset=0)
        wb_w = tile("wb_w", [P, N], U32)
        wb_s = tile("wb_s", [P, N], U8)
        board = [tile("board%d" % t, [P, C], F32) for t in range(PACK)]

        nc.vector.memset(xt_s[:].bitcast(I32), 0)
        nc.vector.memset(wb_s[:].bitcast(I32), 0)
        for t in range(PACK):
            (nc.vector if t < 2 else nc.gpsimd).memset(board[t][:], 0.0)

        nc.sync.dma_start(out=l1[:], in_=offs)
        nc.sync.dma_start(out=wt_w[:].bitcast(I32), in_=wt_words[0].bitcast(I32))
        load_scale_window((nc.sync,), wt_s, wt_scales)
        nc.sync.dma_start(out=l2[:], in_=offs2)
        nc.sync.dma_start(out=xt_w[:].bitcast(I32), in_=xt_words[0].rearrange("p n t -> p (n t)").bitcast(I32))
        load_scale_rows(nc.sync, xt_s, xt_scales)
        nc.sync.dma_start(out=l3[:], in_=offs3)
        nc.sync.dma_start(out=l4[:], in_=offs4)
        nc.sync.dma_start(out=l5[:], in_=offs5)
        nc.sync.dma_start(out=wb_w[:].bitcast(I32), in_=wb_words[0].rearrange("p n t -> p (n t)").bitcast(I32))
        load_scale_rows(nc.sync, wb_s, wb_scales)

        wg_s = tile("wg_s", [P, R], U8)
        wg_w = tile("wg_w", [P, R], U16)
        xg_w = tile("xg_w", [P, J], U32)
        xg_s = tile("xg_s", [P, J], U8)

        hc = HALF // 16

        def deal(dst, src, run, ts):
            nc.vector.tensor_copy(
                out=dst[:].rearrange("p (t b i) -> p b t i", b=P // run, i=run),
                in_=src[:].rearrange("p (b i t) -> p b t i", t=PACK, i=run)[:, :, ts, :],
            )

        nc.vector.tensor_copy(out=wg_w[:], in_=wt_w[:].indirect(l1[:]))
        nc.vector.tensor_copy(out=wg_s[:], in_=wt_s[:].indirect(l1[:]))
        wd0_s = tile("wd0_s", [P, P], U8)
        wd0_w = tile("wd0_w", [P, P], U16)
        deal(wd0_w, wg_w, 8, slice(0, 1))
        deal(wd0_s, wg_s, 16, slice(0, 1))
        nc.vector.tensor_copy(out=xg_w[:], in_=xt_w[:].indirect(l2[:]))
        for h in range(2):
            nc.vector.tensor_copy(out=xg_s[:, h * HALF : (h + 1) * HALF], in_=xt_s[:].indirect(l2[:, h * hc : (h + 1) * hc]))
        others = (PACK - 1) * P
        wdr_s = reuse.tile([P, others], U8, name="wdr_s", align_bytes=64, offset=0)
        wdr_w = reuse.tile([P, others], U16, name="wdr_w", align_bytes=64, offset=others)
        deal(wdr_s, wg_s, 16, slice(1, PACK))
        deal(wdr_w, wg_w, 8, slice(1, PACK))
        wd_s = [wd0_s[:]] + [wdr_s[:, t * P : (t + 1) * P] for t in range(PACK - 1)]
        wd_w = [wd0_w[:]] + [wdr_w[:, t * P : (t + 1) * P] for t in range(PACK - 1)]

        def first_product(bank, t, cols):
            nc.tensor.matmul_mx(
                out=bank,
                lhsT=wd_w[t].bitcast(E2M1),
                lhsT_scale=wd_s[t],
                rhs=xg_w[:, cols].bitcast(E4M3),
                rhs_scale=xg_s[:, cols],
                start=True,
                stop=True,
            )

        a0 = tile("a0", [P, J], F32)
        head = tile("head", [P, HALF], F32, tag="later")
        banks = [ps.tile([P, HALF], F32, name="a0h%d" % h) for h in range(2)]
        for h in range(2):
            first_product(banks[h][:], 0, slice(h * HALF, (h + 1) * HALF))
        nc.scalar.copy(out=head[:], in_=banks[0][:])
        nc.scalar.activation(out=board[0][:].indirect(l3[:, :hc]), in_=head[:], func=ACT.Copy)
        nc.vector.tensor_copy(out=a0[:, HALF:], in_=banks[1][:])
        nc.scalar.activation(out=board[0][:].indirect(l3[:, hc:]), in_=a0[:, HALF:], func=ACT.Copy)
        nc.vector.tensor_copy(out=a0[:, :HALF], in_=banks[0][:])
        rest = tile("rest", [P, PACK - 1, J], F32, tag="later")
        a = [a0[:]] + [rest[:, t, :] for t in range(PACK - 1)]
        for t in range(1, PACK):
            bank = ps.tile([P, J], F32, name="a%d" % t)
            first_product(bank[:], t, slice(0, J))
            nc.vector.tensor_copy(out=a[t], in_=bank[:])
            nc.scalar.activation(out=board[t][:].indirect(l3[:]), in_=a[t], func=ACT.Copy)

        mag = tile("mag", [P, PACK, 2, J], F32)
        last = PACK - 1

        def differences(dst, t, h0, h1):
            for s, lst in enumerate((l4, l5)):
                nc.vector.tensor_tensor(
                    out=dst[:, s, h0 * HALF : h1 * HALF],
                    in0=board[t][:].indirect(lst[:, h0 * hc : h1 * hc]),
                    in1=a[t][:, h0 * HALF : h1 * HALF],
                    op=ALU.subtract,
                )

        diff0 = tile("diff0", [P, 2, J], F32, tag="diff")
        differences(diff0, 0, 0, 2)
        flat = diff0[:].rearrange("p s j -> p (s j)")
        nc.vector.scalar_tensor_tensor(
            out=mag[:, 0].rearrange("p s j -> p (s j)"), in0=flat, scalar=-1.0, in1=flat, op0=ALU.mult, op1=ALU.max
        )
        diffs = tile("diffs", [P, PACK - 1, 2, J], F32, tag="diff")
        for t in (1, 2):
            differences(diffs[:, t - 1], t, 0, 2)
        for h in range(2):
            cols = slice(h * HALF, (h + 1) * HALF)
            differences(diffs[:, last - 1], last, h, h + 1)
            nc.scalar.activation(out=mag[:, 1:last, :, cols], in_=diffs[:, : last - 1, :, cols], func=ACT.Abs)
            nc.scalar.activation(out=mag[:, last, :, cols], in_=diffs[:, last - 1, :, cols], func=ACT.Abs)

        out_v = out.rearrange("(g p) j -> p g j", p=P)
        for h in range(2):
            hid = tile("hid%d" % h, [P, HALF * PACK], BF16)
            near = [
                mag[:, :, s, h * HALF : (h + 1) * HALF].rearrange("p t (b i) -> p b t i", i=4) for s in range(2)
            ]
            nc.vector.tensor_tensor(
                out=hid[:].rearrange("p (b i t) -> p b t i", t=PACK, i=4), in0=near[0], in1=near[1], op=ALU.min
            )
            hq_w = tile("hq_w%d" % h, [P, HALF], U32)
            hq_s = tile("hq_s%d" % h, [P, HALF], U8)
            nc.vector.quantize_mx(out=hq_w[:].bitcast(E4M3), scales=hq_s[:], in_=hid[:])
            for g in range(2):
                res = tile("res%d%d" % (h, g), [P, HALF], F32)
                bank = ps.tile([P, HALF], F32, name=("a0h0", "a0h1", "o0", "o1")[2 * h + g])
                nc.tensor.matmul_mx(
                    out=bank[:],
                    lhsT=wb_w[:, g * P : (g + 1) * P].bitcast(E5M2),
                    lhsT_scale=wb_s[:, g * P : (g + 1) * P],
                    rhs=hq_w[:].bitcast(E4M3),
                    rhs_scale=hq_s[:],
                    start=True,
                    stop=True,
                )
                if h == 1 and g == 0:
                    nc.vector.tensor_copy(out=res[:], in_=bank[:])
                else:
                    nc.scalar.copy(out=res[:], in_=bank[:])
                (nc.sync if g == 0 else nc.scalar).dma_start(out=out_v[:, g, h * HALF : (h + 1) * HALF], in_=res[:])
